import numpy as np
import ml_dtypes


def mxq(x, axis, fmt="e4m3"):
    dtype, down = {"e4m3": (ml_dtypes.float8_e4m3fn, 7), "e5m2": (ml_dtypes.float8_e5m2, 14)}[fmt]
    v = np.moveaxis(np.asarray(x, np.float32).astype(ml_dtypes.bfloat16).astype(np.float64), axis, -1)
    blocks = v.reshape(v.shape[:-1] + (-1, 32))
    amax = np.abs(blocks).max(-1, keepdims=True)
    byte = np.maximum(np.where(amax > 0, np.frexp(amax)[1] - 1 + 127, 0) - down, 1)
    scale = np.exp2(byte - 127.0)
    codes = (blocks / scale).astype(np.float32).astype(dtype).astype(np.float64)
    return np.moveaxis((codes * scale).reshape(v.shape), -1, axis)


WIDE = False


def mx_kscale(k):
    if not WIDE:
        return np.ones(k)
    levels = np.array([10, -10, 5, -5, 0])
    if k % 512:
        return np.exp2(np.random.permutation(np.resize(levels, k // 32))).repeat(32)
    a = np.empty((k // 512, 16))
    for p in range(k // 512):
        a[p, :8] = np.random.permutation(np.resize(levels, 8))
        for g in range(8):
            far = levels[np.abs(levels - a[p, g]) >= 10]
            a[p, g + 8] = far[np.random.randint(len(far))]
    return np.exp2(a.ravel()).repeat(32)


def f64(x):
    return np.asarray(x).astype(np.float64)


def striped8(idx):
    return np.asarray(idx).reshape(8, -1, 16).transpose(0, 2, 1).reshape(128, -1).astype(np.uint16)


def unstriped8(offs):
    return offs.reshape(8, 16, -1).transpose(0, 2, 1).reshape(8, -1).astype(np.int64)


def pick8(x, idx, run):
    r = np.arange(len(x))
    return x[r[:, None], idx[r % (8 * run) // run]]


E2M1 = np.array([0.0, 0.5, 1.0, 1.5, 2.0, 3.0, 4.0, 6.0, -0.0, -0.5, -1.0, -1.5, -2.0, -3.0, -4.0, -6.0])


def pack_weight(w, fmt):
    k, n = w.shape
    w = f64(np.asarray(w, np.float32).astype(ml_dtypes.bfloat16)).reshape(k // 32, 32, n)
    amax = np.abs(w).max(1)
    if fmt == "e4m3":
        byte = np.frexp(amax)[1] - 1 + 127 - 7
    else:
        mant, ex = np.frexp(amax / 6.0)
        byte = np.where(mant > 0.5, ex, ex - 1) + 127
    byte = np.clip(np.where(amax > 0, byte, 1), 1, 254)
    scaled = (w * np.exp2(127.0 - byte)[:, None, :]).reshape(k, n).astype(np.float32)
    by_word = np.ascontiguousarray(scaled.reshape(k // 512, 128, 4, n).transpose(0, 1, 3, 2))
    if fmt == "e4m3":
        words = by_word.astype(ml_dtypes.float8_e4m3fn).view(np.uint8)
    else:
        c = by_word.astype(ml_dtypes.float4_e2m1fn).view(np.uint8) & 0xF
        words = (c[..., 0::2] | (c[..., 1::2] << 4)).reshape(k // 512, 128, 2 * n)
    return np.ascontiguousarray(words), np.ascontiguousarray(byte.astype(np.uint8).reshape(k // 512, 16, n))


def unpack_weight(words, scales, fmt):
    g, _, n = scales.shape
    words = np.ascontiguousarray(words).reshape(g, 128, n, -1)
    if fmt == "e4m3":
        vals = words.view(ml_dtypes.float8_e4m3fn).astype(np.float64)
    else:
        nib = np.empty((g, 128, n, 4), np.uint8)
        nib[..., 0::2] = words & 0xF
        nib[..., 1::2] = words >> 4
        vals = E2M1[nib]
    vals = vals * np.repeat(np.exp2(scales.astype(np.float64) - 127.0), 8, axis=1)[..., None]
    return vals.transpose(0, 1, 3, 2).reshape(g * 512, n)


D, V, Q, I, G = 512, 2048, 128, 512, 64


def setup_inputs():
    n = np.random.standard_normal
    idx = np.stack([np.random.permutation(V)[:I] for _ in range(8)])
    fd = mx_kscale(D)
    vocp = pack_weight(n((D, V)) / fd[:, None], "e2m1")
    return {
        "hid": (n((D, Q)) * 1.0 / np.sqrt(D) * fd[:, None]).astype(np.float32),
        "voc_words": vocp[0],
        "voc_scales": vocp[1],
        "target": (np.random.uniform(0.0, 0.1, (Q, G))).astype(np.float32),
        "old": (0.5 * n((Q, V))).astype(np.float32),
        "offs": striped8(idx),
    }


def reference(hid, voc_words, voc_scales, target, old, offs):
    idx = unstriped8(offs)
    vocu = unpack_weight(voc_words, voc_scales, "e2m1")
    hidq = mxq(f64(hid), 0, "e4m3")
    a = hidq.T @ vocu
    m1 = np.max(a, axis=1, keepdims=True)
    p = np.exp(a - m1)
    z = np.sum(p, axis=1, keepdims=True)
    px = np.exp(pick8(a, idx, 16) - m1)
    u1 = px.reshape(Q, G, I // G).sum(axis=2) / z
    du1 = f64(target) / u1
    e1 = du1 / z
    r1 = np.repeat(e1, I // G, axis=1)
    dz = np.sum(du1 * px.reshape(Q, G, I // G).sum(axis=2) / np.square(z) * (-1.0), axis=1, keepdims=True)
    e2 = r1 * px
    s2 = np.zeros((Q, V))
    s2[np.arange(Q)[:, None], idx[np.arange(Q) % 128 // 16]] = e2
    da = dz * p + s2
    y = da * 64.0 + f64(old)
    return y

@@ -1,0 +1,195 @@
+from contextlib import ExitStack
+
+import concourse.mybir as mybir
+from concourse.masks import make_identity
+
+D, V, Q, I, G = 512, 2048, 128, 512, 64
+FLOPS = 2 * D * Q * V
+
+F32 = mybir.dt.float32
+BF16 = mybir.dt.bfloat16
+I32 = mybir.dt.int32
+U32 = mybir.dt.uint32
+U16 = mybir.dt.uint16
+U8 = mybir.dt.uint8
+FP8X4 = mybir.dt.float8_e4m3fn_x4
+FP4X4 = mybir.dt.float4_e2m1fn_x4
+ALU = mybir.AluOpType
+ACT = mybir.ActivationFunctionType
+AXIS_X = mybir.AxisListType.X
+
+P = 128
+PACK = 4
+BANK = 512
+BANKS = V // BANK
+RUN = I // G
+HALVES = 2
+STORE_WIDTHS = (128, 384, 512, 512, 384, 128)
+
+
+def tile_attend_bgroupshare_heads_kernel(tc, hid, voc_words, voc_scales, target, old, offs, out):
+    nc = tc.nc
+    with ExitStack() as ctx:
+        sb = ctx.enter_context(tc.tile_pool(name="sb", bufs=1))
+        ps = ctx.enter_context(tc.psum_pool(name="ps", bufs=1))
+
+        offsets = sb.tile([P, I // 16], U16, name="offsets")
+        voc_plane = sb.tile([P, V], U8, name="voc_plane", align_bytes=64)
+        nc.vector.memset(voc_plane[:].bitcast(I32), 0)
+
+        hid_raw = sb.tile([P, PACK, Q], F32, name="hid_raw")
+        nc.sync.dma_start(out=hid_raw[:], in_=hid.rearrange("(p j) q -> p j q", j=PACK))
+        words_hbm = voc_words[0].bitcast(I32)
+        voc_codes = [sb.tile([P, V], U8, name="voc_codes%d" % h, align_bytes=64) for h in range(2)]
+        nc.sync.dma_start(out=voc_codes[0][:].bitcast(I32), in_=words_hbm[:, 0 : V // 4])
+        for quad in range(4):
+            nc.sync.dma_start(
+                out=voc_plane[32 * quad : 32 * quad + 4, :].bitcast(I32),
+                in_=voc_scales[0, 4 * quad : 4 * quad + 4, :].bitcast(I32),
+            )
+        nc.sync.dma_start(out=voc_codes[1][:].bitcast(I32), in_=words_hbm[:, V // 4 : V // 2])
+        target_sb = sb.tile([P, G], F32, name="target_sb")
+        nc.sync.dma_start(out=target_sb[:], in_=target)
+        nc.sync.dma_start(offsets[:], offs)
+        old_sb = [sb.tile([P, BANK], F32, name="old_sb%d" % b) for b in range(BANKS)]
+        for b in range(BANKS):
+            nc.sync.dma_start(out=old_sb[b][:], in_=old[:, b * BANK : (b + 1) * BANK])
+
+        listed = sb.tile([P, V], F32, name="listed")
+        nc.vector.memset(listed[:], 0.0)
+
+        hid_bf = sb.tile([P, Q, PACK], BF16, name="hid_bf", align_bytes=64)
+        nc.vector.tensor_copy(
+            out=hid_bf[:].rearrange("p (c i) j -> p c j i", i=4),
+            in_=hid_raw[:].rearrange("p j (c i) -> p c j i", i=4),
+        )
+        hid_codes = sb.tile([P, Q], U32, name="hid_codes", align_bytes=64)
+        hid_plane = sb.tile([P, Q], U8, name="hid_plane", align_bytes=64)
+        nc.vector.quantize_mx(
+            out=hid_codes[:].bitcast(FP8X4), scales=hid_plane[:], in_=hid_bf[:].rearrange("p q j -> p (q j)")
+        )
+
+        slot_target = sb.tile([P, G, RUN], F32, name="slot_target")
+        slot_target_sum = sb.tile([P, 1], F32, name="slot_target_sum")
+        nc.scalar.activation(
+            out=slot_target[:], in_=target_sb[:].unsqueeze(2).to_broadcast([P, G, RUN]), func=ACT.Copy, scale=64.0,
+            accum_out=slot_target_sum[:],
+        )
+
+        scores = sb.tile([P, V], F32, name="scores")
+        bank_max = sb.tile([P, BANKS], F32, name="bank_max")
+        neg_shift = sb.tile([P, BANKS, 8], F32, name="neg_shift")
+        neg_max = neg_shift[:, BANKS - 1, 0:1]
+        bank_sum = sb.tile([P, BANKS], F32, name="bank_sum")
+        bank_exp = [sb.tile([P, BANK], F32, name="bank_exp%d" % b) for b in range(BANKS)]
+        for b in range(BANKS):
+            cols = slice(b * BANK, (b + 1) * BANK)
+            acc = ps.tile([P, BANK], F32, name="acc%d" % b, tag="acc%d" % b)
+            first = (b % 2) * 2 * BANK
+            nc.tensor.matmul_mx(
+                out=acc[:],
+                lhsT=hid_codes[:].bitcast(FP8X4),
+                lhsT_scale=hid_plane[:],
+                rhs=voc_codes[b // 2][:, first : first + 2 * BANK].bitcast(FP4X4),
+                rhs_scale=voc_plane[:, cols],
+                start=True,
+                stop=True,
+            )
+            nc.vector.tensor_scalar(
+                out=scores[:, cols], in0=acc[:], scalar1=1.0, scalar2=None, op0=ALU.mult, op1=ALU.max,
+                accum_out=bank_max[:, b : b + 1],
+            )
+            if b < BANKS - 1:
+                nc.gpsimd.tensor_scalar(
+                    out=neg_shift[:, b, 0:1], in0=bank_max[:, b : b + 1], scalar1=-1.0, scalar2=0.0,
+                    op0=ALU.mult, op1=ALU.add,
+                )
+            else:
+                nc.vector.tensor_reduce(out=neg_max, in_=bank_max[:], axis=AXIS_X, op=ALU.max, negate=True)
+            nc.scalar.activation(
+                out=bank_exp[b][:], in_=scores[:, cols], func=ACT.Exp, bias=neg_shift[:, b, 0:1],
+                accum_out=bank_sum[:, b : b + 1],
+            )
+
+        picked = sb.tile([P, I], F32, name="picked")
+        nc.vector.tensor_copy(out=picked[:], in_=scores[:].indirect(offsets[:]))
+
+        bank_factor = sb.tile([P, BANKS], F32, name="bank_factor")
+        nc.scalar.activation(out=bank_factor[:], in_=neg_shift[:, :, 0], func=ACT.Exp, scale=-1.0, bias=neg_max)
+
+        gh = G // HALVES
+        ih = I // HALVES
+        px = sb.tile([P, I], F32, name="px")
+        for h in range(HALVES):
+            nc.scalar.activation(out=px[:, h * ih : (h + 1) * ih], in_=picked[:, h * ih : (h + 1) * ih], func=ACT.Exp, bias=neg_max)
+
+        weighted = sb.tile([P, BANKS], F32, name="weighted")
+        z = sb.tile([P, 1], F32, name="z")
+        nc.vector.scalar_tensor_tensor(
+            out=weighted[:], in0=bank_factor[:], scalar=-float(RUN), in1=bank_sum[:], op0=ALU.mult, op1=ALU.mult, accum_out=z[:]
+        )
+        group_sum = [sb.tile([P, gh], F32, name="group_sum%d" % h) for h in range(HALVES)]
+        nc.vector.tensor_reduce(
+            out=group_sum[0][:], in_=px[:, 0:ih].rearrange("p (g r) -> p g r", r=RUN), axis=AXIS_X, op=ALU.add
+        )
+        inv_z = sb.tile([P, 1], F32, name="inv_z")
+        nc.vector.reciprocal(out=inv_z[:], in_=z[:])
+        nc.vector.tensor_reduce(
+            out=group_sum[1][:], in_=px[:, ih:I].rearrange("p (g r) -> p g r", r=RUN), axis=AXIS_X, op=ALU.add
+        )
+        coef = sb.tile([P, BANKS], F32, name="coef")
+        nc.vector.tensor_scalar(
+            out=coef[:], in0=bank_factor[:], scalar1=inv_z[:], scalar2=slot_target_sum[:], op0=ALU.mult, op1=ALU.mult
+        )
+        ident = sb.tile([P, P], F32, name="ident")
+        make_identity(nc, ident[:])
+        blocks = [slice(j * P, (j + 1) * P) for j in range(BANK // P)]
+        turned = []
+        for b in range(BANKS):
+            t_ps = ps.tile([P, BANK], F32, name="turned%d" % b)
+            for j, blk in enumerate(blocks):
+                nc.tensor.matmul(out=t_ps[:, blk], lhsT=old_sb[b][:, blk], rhs=ident[:], is_transpose=True, start=(j == 0), stop=False)
+            turned.append(t_ps)
+
+        def scale_and_turn(b):
+            scaled = sb.tile([P, BANK], F32, name="scaled%d" % b)
+            nc.scalar.activation(out=scaled[:], in_=bank_exp[b][:], func=ACT.Copy, scale=coef[:, b : b + 1])
+            for j, blk in enumerate(blocks):
+                nc.tensor.matmul(out=turned[b][:, blk], lhsT=scaled[:, blk], rhs=ident[:], is_transpose=True, start=False, stop=(j == len(blocks) - 1))
+
+        def turn_back(b):
+            turned_sb = sb.tile([P, BANK], F32, name="turned_sb%d" % b)
+            nc.scalar.copy(out=turned_sb[:], in_=turned[b][:])
+            dense = ps.tile([P, BANK], F32, name="dense%d" % b, tag="acc%d" % b)
+            for blk in blocks:
+                nc.tensor.transpose(dense[:, blk], turned_sb[:, blk], ident[:])
+            return dense
+
+        inv_group = [sb.tile([P, gh], F32, name="inv_group%d" % h) for h in range(HALVES)]
+        for h in range(HALVES):
+            nc.vector.reciprocal(out=inv_group[h][:], in_=group_sum[h][:])
+        r1 = sb.tile([P, G, RUN], F32, name="r1")
+        for h in range(HALVES):
+            groups = slice(h * gh, (h + 1) * gh)
+            nc.vector.tensor_tensor(
+                out=r1[:, groups, :], in0=slot_target[:, groups, :],
+                in1=inv_group[h][:].unsqueeze(2).to_broadcast([P, gh, RUN]), op=ALU.mult,
+            )
+        nc.vector.tensor_tensor(
+            out=listed[:].indirect(offsets[:]), in0=px[:], in1=r1[:].rearrange("p g r -> p (g r)"), op=ALU.mult
+        )
+        scale_and_turn(0)
+        scale_and_turn(1)
+        base = []
+        for b in range(BANKS):
+            base.append(turn_back(b))
+            if b + 2 < BANKS:
+                scale_and_turn(b + 2)
+        start = 0
+        for n, width in enumerate(STORE_WIDTHS):
+            b, first = divmod(start, BANK)
+            cols = slice(start, start + width)
+            result = sb.tile([P, width], F32, name="result%d" % n)
+            nc.vector.tensor_tensor(out=result[:], in0=base[b][:, first : first + width], in1=listed[:, cols], op=ALU.add)
+            nc.sync.dma_start(out=out[:, cols], in_=result[:])
+            start = start + width

@@ -24,7 +24,6 @@ BANK = 512
 BANKS = V // BANK
 RUN = I // G
 HALVES = 2
-STORE_WIDTHS = (128, 384, 512, 512, 384, 128)
 
 
 def tile_attend_bgroupshare_heads_kernel(tc, hid, voc_words, voc_scales, target, old, offs, out):
@@ -78,8 +77,11 @@ def tile_attend_bgroupshare_heads_kernel(tc, hid, voc_words, voc_scales, target,
 
         scores = sb.tile([P, V], F32, name="scores")
         bank_max = sb.tile([P, BANKS], F32, name="bank_max")
-        neg_shift = sb.tile([P, BANKS, 8], F32, name="neg_shift")
-        neg_max = neg_shift[:, BANKS - 1, 0:1]
+        slots = sb.tile([P, I + 8], F32, name="slots")
+        px = slots[:, 0:I]
+        neg_shift = slots[:, 0 : 8 * BANKS : 8]
+        neg_max = slots[:, I : I + 1]
+        last_shift = 8 * (BANKS - 1)
         bank_sum = sb.tile([P, BANKS], F32, name="bank_sum")
         bank_exp = [sb.tile([P, BANK], F32, name="bank_exp%d" % b) for b in range(BANKS)]
         for b in range(BANKS):
@@ -101,13 +103,13 @@ def tile_attend_bgroupshare_heads_kernel(tc, hid, voc_words, voc_scales, target,
             )
             if b < BANKS - 1:
                 nc.gpsimd.tensor_scalar(
-                    out=neg_shift[:, b, 0:1], in0=bank_max[:, b : b + 1], scalar1=-1.0, scalar2=0.0,
+                    out=neg_shift[:, b : b + 1], in0=bank_max[:, b : b + 1], scalar1=-1.0, scalar2=0.0,
                     op0=ALU.mult, op1=ALU.add,
                 )
             else:
-                nc.vector.tensor_reduce(out=neg_max, in_=bank_max[:], axis=AXIS_X, op=ALU.max, negate=True)
+                nc.vector.tensor_reduce(out=slots[:, last_shift : I + 1 : I - last_shift], in_=bank_max[:].unsqueeze(1).to_broadcast([P, 2, BANKS]), axis=AXIS_X, op=ALU.max, negate=True)
             nc.scalar.activation(
-                out=bank_exp[b][:], in_=scores[:, cols], func=ACT.Exp, bias=neg_shift[:, b, 0:1],
+                out=bank_exp[b][:], in_=scores[:, cols], func=ACT.Exp, bias=neg_shift[:, b : b + 1],
                 accum_out=bank_sum[:, b : b + 1],
             )
 
@@ -115,11 +117,10 @@ def tile_attend_bgroupshare_heads_kernel(tc, hid, voc_words, voc_scales, target,
         nc.vector.tensor_copy(out=picked[:], in_=scores[:].indirect(offsets[:]))
 
         bank_factor = sb.tile([P, BANKS], F32, name="bank_factor")
-        nc.scalar.activation(out=bank_factor[:], in_=neg_shift[:, :, 0], func=ACT.Exp, scale=-1.0, bias=neg_max)
+        nc.scalar.activation(out=bank_factor[:], in_=neg_shift, func=ACT.Exp, scale=-1.0, bias=neg_max)
 
         gh = G // HALVES
         ih = I // HALVES
-        px = sb.tile([P, I], F32, name="px")
         for h in range(HALVES):
             nc.scalar.activation(out=px[:, h * ih : (h + 1) * ih], in_=picked[:, h * ih : (h + 1) * ih], func=ACT.Exp, bias=neg_max)
 
@@ -132,7 +133,7 @@ def tile_attend_bgroupshare_heads_kernel(tc, hid, voc_words, voc_scales, target,
         nc.vector.tensor_reduce(
             out=group_sum[0][:], in_=px[:, 0:ih].rearrange("p (g r) -> p g r", r=RUN), axis=AXIS_X, op=ALU.add
         )
-        inv_z = sb.tile([P, 1], F32, name="inv_z")
+        inv_z = sb.tile([P, 1], F32, name="inv_z", tag="half0")
         nc.vector.reciprocal(out=inv_z[:], in_=z[:])
         nc.vector.tensor_reduce(
             out=group_sum[1][:], in_=px[:, ih:I].rearrange("p (g r) -> p g r", r=RUN), axis=AXIS_X, op=ALU.add
@@ -145,7 +146,7 @@ def tile_attend_bgroupshare_heads_kernel(tc, hid, voc_words, voc_scales, target,
         make_identity(nc, ident[:])
         blocks = [slice(j * P, (j + 1) * P) for j in range(BANK // P)]
         turned = []
-        for b in range(BANKS):
+        for b in range(BANKS - 1):
             t_ps = ps.tile([P, BANK], F32, name="turned%d" % b)
             for j, blk in enumerate(blocks):
                 nc.tensor.matmul(out=t_ps[:, blk], lhsT=old_sb[b][:, blk], rhs=ident[:], is_transpose=True, start=(j == 0), stop=False)
@@ -165,7 +166,7 @@ def tile_attend_bgroupshare_heads_kernel(tc, hid, voc_words, voc_scales, target,
                 nc.tensor.transpose(dense[:, blk], turned_sb[:, blk], ident[:])
             return dense
 
-        inv_group = [sb.tile([P, gh], F32, name="inv_group%d" % h) for h in range(HALVES)]
+        inv_group = [sb.tile([P, gh], F32, name="inv_group%d" % h, tag="half%d" % h) for h in range(HALVES)]
         for h in range(HALVES):
             nc.vector.reciprocal(out=inv_group[h][:], in_=group_sum[h][:])
         r1 = sb.tile([P, G, RUN], F32, name="r1")
@@ -176,20 +177,28 @@ def tile_attend_bgroupshare_heads_kernel(tc, hid, voc_words, voc_scales, target,
                 in1=inv_group[h][:].unsqueeze(2).to_broadcast([P, gh, RUN]), op=ALU.mult,
             )
         nc.vector.tensor_tensor(
-            out=listed[:].indirect(offsets[:]), in0=px[:], in1=r1[:].rearrange("p g r -> p (g r)"), op=ALU.mult
+            out=listed[:].indirect(offsets[:]), in0=px, in1=r1[:].rearrange("p g r -> p (g r)"), op=ALU.mult
         )
-        scale_and_turn(0)
-        scale_and_turn(1)
-        base = []
-        for b in range(BANKS):
-            base.append(turn_back(b))
-            if b + 2 < BANKS:
-                scale_and_turn(b + 2)
-        start = 0
-        for n, width in enumerate(STORE_WIDTHS):
-            b, first = divmod(start, BANK)
+        for b in range(BANKS - 1):
+            scale_and_turn(b)
+        base = [turn_back(b) for b in range(BANKS - 1)]
+        last = BANKS - 1
+        dense_last = []
+        for h in range(2):
+            half = slice(h * BANK // 2, (h + 1) * BANK // 2)
+            dense_half = sb.tile([P, BANK // 2], F32, name="dense_half%d" % h, tag="half%d" % h)
+            dense_last.append(dense_half)
+            nc.vector.scalar_tensor_tensor(
+                out=dense_half[:], in0=bank_exp[last][:, half], scalar=coef[:, last : last + 1],
+                in1=old_sb[last][:, half], op0=ALU.mult, op1=ALU.add,
+            )
+        pieces = [(last * BANK, dense_last[0][:, 0:P]), (last * BANK + P, dense_last[0][:, P : 2 * P]), (last * BANK + 2 * P, dense_last[1][:])]
+        pieces.extend((b * BANK, base[b][:]) for b in range(BANKS - 2))
+        pieces.append(((BANKS - 2) * BANK, base[BANKS - 2][:, 0 : 3 * P]))
+        pieces.append(((BANKS - 2) * BANK + 3 * P, base[BANKS - 2][:, 3 * P : BANK]))
+        for n, (start, dense) in enumerate(pieces):
+            width = dense.shape[1]
             cols = slice(start, start + width)
             result = sb.tile([P, width], F32, name="result%d" % n)
-            nc.vector.tensor_tensor(out=result[:], in0=base[b][:, first : first + width], in1=listed[:, cols], op=ALU.add)
+            nc.vector.tensor_tensor(out=result[:], in0=dense, in1=listed[:, cols], op=ALU.add)
             nc.sync.dma_start(out=out[:, cols], in_=result[:])
-            start = start + width

from contextlib import ExitStack

import concourse.mybir as mybir
from concourse.masks import make_identity

D, V, Q, I, G = 512, 2048, 128, 512, 64
FLOPS = 2 * D * Q * V

F32 = mybir.dt.float32
BF16 = mybir.dt.bfloat16
I32 = mybir.dt.int32
U32 = mybir.dt.uint32
U16 = mybir.dt.uint16
U8 = mybir.dt.uint8
FP8X4 = mybir.dt.float8_e4m3fn_x4
FP4X4 = mybir.dt.float4_e2m1fn_x4
ALU = mybir.AluOpType
ACT = mybir.ActivationFunctionType
AXIS_X = mybir.AxisListType.X

P = 128
PACK = 4
BANK = 512
BANKS = V // BANK
RUN = I // G
HALVES = 2


def tile_attend_bgroupshare_heads_kernel(tc, hid, voc_words, voc_scales, target, old, offs, out):
    nc = tc.nc
    with ExitStack() as ctx:
        sb = ctx.enter_context(tc.tile_pool(name="sb", bufs=1))
        ps = ctx.enter_context(tc.psum_pool(name="ps", bufs=1))

        offsets = sb.tile([P, I // 16], U16, name="offsets")
        voc_plane = sb.tile([P, V], U8, name="voc_plane", align_bytes=64)
        nc.vector.memset(voc_plane[:].bitcast(I32), 0)

        hid_raw = sb.tile([P, PACK, Q], F32, name="hid_raw")
        nc.sync.dma_start(out=hid_raw[:], in_=hid.rearrange("(p j) q -> p j q", j=PACK))
        words_hbm = voc_words[0].bitcast(I32)
        voc_codes = [sb.tile([P, V], U8, name="voc_codes%d" % h, align_bytes=64) for h in range(2)]
        nc.sync.dma_start(out=voc_codes[0][:].bitcast(I32), in_=words_hbm[:, 0 : V // 4])
        for quad in range(4):
            nc.sync.dma_start(
                out=voc_plane[32 * quad : 32 * quad + 4, :].bitcast(I32),
                in_=voc_scales[0, 4 * quad : 4 * quad + 4, :].bitcast(I32),
            )
        nc.sync.dma_start(out=voc_codes[1][:].bitcast(I32), in_=words_hbm[:, V // 4 : V // 2])
        target_sb = sb.tile([P, G], F32, name="target_sb")
        nc.sync.dma_start(out=target_sb[:], in_=target)
        nc.sync.dma_start(offsets[:], offs)
        old_sb = [sb.tile([P, BANK], F32, name="old_sb%d" % b) for b in range(BANKS)]
        for b in range(BANKS):
            nc.sync.dma_start(out=old_sb[b][:], in_=old[:, b * BANK : (b + 1) * BANK])

        listed = sb.tile([P, V], F32, name="listed")
        nc.vector.memset(listed[:], 0.0)

        hid_bf = sb.tile([P, Q, PACK], BF16, name="hid_bf", align_bytes=64)
        nc.vector.tensor_copy(
            out=hid_bf[:].rearrange("p (c i) j -> p c j i", i=4),
            in_=hid_raw[:].rearrange("p j (c i) -> p c j i", i=4),
        )
        hid_codes = sb.tile([P, Q], U32, name="hid_codes", align_bytes=64)
        hid_plane = sb.tile([P, Q], U8, name="hid_plane", align_bytes=64)
        nc.vector.quantize_mx(
            out=hid_codes[:].bitcast(FP8X4), scales=hid_plane[:], in_=hid_bf[:].rearrange("p q j -> p (q j)")
        )

        slot_target = sb.tile([P, G, RUN], F32, name="slot_target")
        slot_target_sum = sb.tile([P, 1], F32, name="slot_target_sum")
        nc.scalar.activation(
            out=slot_target[:], in_=target_sb[:].unsqueeze(2).to_broadcast([P, G, RUN]), func=ACT.Copy, scale=64.0,
            accum_out=slot_target_sum[:],
        )

        scores = sb.tile([P, V], F32, name="scores")
        bank_max = sb.tile([P, BANKS], F32, name="bank_max")
        slots = sb.tile([P, I + 8], F32, name="slots")
        px = slots[:, 0:I]
        neg_shift = slots[:, 0 : 8 * BANKS : 8]
        neg_max = slots[:, I : I + 1]
        last_shift = 8 * (BANKS - 1)
        bank_sum = sb.tile([P, BANKS], F32, name="bank_sum")
        bank_exp = [sb.tile([P, BANK], F32, name="bank_exp%d" % b) for b in range(BANKS)]
        for b in range(BANKS):
            cols = slice(b * BANK, (b + 1) * BANK)
            acc = ps.tile([P, BANK], F32, name="acc%d" % b, tag="acc%d" % b)
            first = (b % 2) * 2 * BANK
            nc.tensor.matmul_mx(
                out=acc[:],
                lhsT=hid_codes[:].bitcast(FP8X4),
                lhsT_scale=hid_plane[:],
                rhs=voc_codes[b // 2][:, first : first + 2 * BANK].bitcast(FP4X4),
                rhs_scale=voc_plane[:, cols],
                start=True,
                stop=True,
            )
            nc.vector.tensor_scalar(
                out=scores[:, cols], in0=acc[:], scalar1=1.0, scalar2=None, op0=ALU.mult, op1=ALU.max,
                accum_out=bank_max[:, b : b + 1],
            )
            if b < BANKS - 1:
                nc.gpsimd.tensor_scalar(
                    out=neg_shift[:, b : b + 1], in0=bank_max[:, b : b + 1], scalar1=-1.0, scalar2=0.0,
                    op0=ALU.mult, op1=ALU.add,
                )
            else:
                nc.vector.tensor_reduce(out=slots[:, last_shift : I + 1 : I - last_shift], in_=bank_max[:].unsqueeze(1).to_broadcast([P, 2, BANKS]), axis=AXIS_X, op=ALU.max, negate=True)
            nc.scalar.activation(
                out=bank_exp[b][:], in_=scores[:, cols], func=ACT.Exp, bias=neg_shift[:, b : b + 1],
                accum_out=bank_sum[:, b : b + 1],
            )

        picked = sb.tile([P, I], F32, name="picked")
        nc.vector.tensor_copy(out=picked[:], in_=scores[:].indirect(offsets[:]))

        bank_factor = sb.tile([P, BANKS], F32, name="bank_factor")
        nc.scalar.activation(out=bank_factor[:], in_=neg_shift, func=ACT.Exp, scale=-1.0, bias=neg_max)

        gh = G // HALVES
        ih = I // HALVES
        for h in range(HALVES):
            nc.scalar.activation(out=px[:, h * ih : (h + 1) * ih], in_=picked[:, h * ih : (h + 1) * ih], func=ACT.Exp, bias=neg_max)

        weighted = sb.tile([P, BANKS], F32, name="weighted")
        z = sb.tile([P, 1], F32, name="z")
        nc.vector.scalar_tensor_tensor(
            out=weighted[:], in0=bank_factor[:], scalar=-float(RUN), in1=bank_sum[:], op0=ALU.mult, op1=ALU.mult, accum_out=z[:]
        )
        group_sum = [sb.tile([P, gh], F32, name="group_sum%d" % h) for h in range(HALVES)]
        nc.vector.tensor_reduce(
            out=group_sum[0][:], in_=px[:, 0:ih].rearrange("p (g r) -> p g r", r=RUN), axis=AXIS_X, op=ALU.add
        )
        inv_z = sb.tile([P, 1], F32, name="inv_z", tag="half0")
        nc.vector.reciprocal(out=inv_z[:], in_=z[:])
        nc.vector.tensor_reduce(
            out=group_sum[1][:], in_=px[:, ih:I].rearrange("p (g r) -> p g r", r=RUN), axis=AXIS_X, op=ALU.add
        )
        coef = sb.tile([P, BANKS], F32, name="coef")
        nc.vector.tensor_scalar(
            out=coef[:], in0=bank_factor[:], scalar1=inv_z[:], scalar2=slot_target_sum[:], op0=ALU.mult, op1=ALU.mult
        )
        ident = sb.tile([P, P], F32, name="ident")
        make_identity(nc, ident[:])
        blocks = [slice(j * P, (j + 1) * P) for j in range(BANK // P)]
        turned = []
        for b in range(BANKS - 1):
            t_ps = ps.tile([P, BANK], F32, name="turned%d" % b)
            for j, blk in enumerate(blocks):
                nc.tensor.matmul(out=t_ps[:, blk], lhsT=old_sb[b][:, blk], rhs=ident[:], is_transpose=True, start=(j == 0), stop=False)
            turned.append(t_ps)

        def scale_and_turn(b):
            scaled = sb.tile([P, BANK], F32, name="scaled%d" % b)
            nc.scalar.activation(out=scaled[:], in_=bank_exp[b][:], func=ACT.Copy, scale=coef[:, b : b + 1])
            for j, blk in enumerate(blocks):
                nc.tensor.matmul(out=turned[b][:, blk], lhsT=scaled[:, blk], rhs=ident[:], is_transpose=True, start=False, stop=(j == len(blocks) - 1))

        def turn_back(b):
            turned_sb = sb.tile([P, BANK], F32, name="turned_sb%d" % b)
            nc.scalar.copy(out=turned_sb[:], in_=turned[b][:])
            dense = ps.tile([P, BANK], F32, name="dense%d" % b, tag="acc%d" % b)
            for blk in blocks:
                nc.tensor.transpose(dense[:, blk], turned_sb[:, blk], ident[:])
            return dense

        inv_group = [sb.tile([P, gh], F32, name="inv_group%d" % h, tag="half%d" % h) for h in range(HALVES)]
        for h in range(HALVES):
            nc.vector.reciprocal(out=inv_group[h][:], in_=group_sum[h][:])
        r1 = sb.tile([P, G, RUN], F32, name="r1")
        for h in range(HALVES):
            groups = slice(h * gh, (h + 1) * gh)
            nc.vector.tensor_tensor(
                out=r1[:, groups, :], in0=slot_target[:, groups, :],
                in1=inv_group[h][:].unsqueeze(2).to_broadcast([P, gh, RUN]), op=ALU.mult,
            )
        nc.vector.tensor_tensor(
            out=listed[:].indirect(offsets[:]), in0=px, in1=r1[:].rearrange("p g r -> p (g r)"), op=ALU.mult
        )
        for b in range(BANKS - 1):
            scale_and_turn(b)
        base = [turn_back(b) for b in range(BANKS - 1)]
        last = BANKS - 1
        dense_last = []
        for h in range(2):
            half = slice(h * BANK // 2, (h + 1) * BANK // 2)
            dense_half = sb.tile([P, BANK // 2], F32, name="dense_half%d" % h, tag="half%d" % h)
            dense_last.append(dense_half)
            nc.vector.scalar_tensor_tensor(
                out=dense_half[:], in0=bank_exp[last][:, half], scalar=coef[:, last : last + 1],
                in1=old_sb[last][:, half], op0=ALU.mult, op1=ALU.add,
            )
        pieces = [(last * BANK, dense_last[0][:, 0:P]), (last * BANK + P, dense_last[0][:, P : 2 * P]), (last * BANK + 2 * P, dense_last[1][:])]
        pieces.extend((b * BANK, base[b][:]) for b in range(BANKS - 2))
        pieces.append(((BANKS - 2) * BANK, base[BANKS - 2][:, 0 : 3 * P]))
        pieces.append(((BANKS - 2) * BANK + 3 * P, base[BANKS - 2][:, 3 * P : BANK]))
        for n, (start, dense) in enumerate(pieces):
            width = dense.shape[1]
            cols = slice(start, start + width)
            result = sb.tile([P, width], F32, name="result%d" % n)
            nc.vector.tensor_tensor(out=result[:], in0=dense, in1=listed[:, cols], op=ALU.add)
            nc.sync.dma_start(out=out[:, cols], in_=result[:])
